import numpy as np, ml_dtypes
CORES = [32,160,288,416,80,208,336,464]
N = 8
T, CAP = 1024, 256
def entries(a): return a.T.reshape(-1)
def pack(v, P): return np.ascontiguousarray(np.asarray(v, np.int32).reshape(-1, P).T)
def lists(rng, how):
    n = rng.integers(1, CAP + 1, N)
    if how == "none": n[rng.integers(N)] = 0; n[rng.integers(N)] = 0
    if how == "full": n[:] = CAP
    if how == "one": n[:] = 1
    if how == "void": n[:] = 0
    Kp = np.zeros((N, T), np.int32)
    for r in range(N): Kp[r, (np.arange(T - n[r], T) if how == "last" else rng.permutation(T)[:n[r]])] = 1
    return {"keep": np.stack([pack(Kp[r], 16) for r in range(N)])}
def setup_inputs(rng):
    return dict({"x": rng.standard_normal((N, 128, T), dtype=np.float32).astype(ml_dtypes.bfloat16)}, **lists(rng, "uniform"))
def setup_inputs_full(rng):
    d = setup_inputs(rng); d.update(lists(rng, "full"))
    for k in ("x",): d[k] = (d[k].astype(np.float32) * 1048576.0).astype(d[k].dtype)
    return d
def setup_inputs_last(rng):
    d = setup_inputs(rng); d.update(lists(rng, "last"))
    for k in ("x",): d[k] = (d[k].astype(np.float32) * (1 / 1024.0)).astype(d[k].dtype)
    return d
def setup_inputs_none(rng):
    d = setup_inputs(rng); d.update(lists(rng, "none"))
    return d
def setup_inputs_one(rng):
    d = setup_inputs(rng); d.update(lists(rng, "one"))
    return d
def setup_inputs_void(rng):
    d = setup_inputs(rng); d.update(lists(rng, "void"))
    return d
def check_inputs(x):
    bad = []
    if x["keep"].min() < 0 or x["keep"].max() >= 2: bad.append("keep out of range")
    if max(int(a.sum()) for a in x["keep"]) > CAP: bad.append("a rank keeps more than CAP")
    return bad
def reference(x, keep):
    kept = np.concatenate([x[r][:, entries(keep[r]) == 1] for r in range(N)], axis=1)
    y = np.zeros((128, N * CAP), x.dtype); y[:, :kept.shape[1]] = kept
    return {"y": np.broadcast_to(y, (N, 128, N * CAP))}

@@ -1,0 +1,219 @@
+from concourse.bass import DstId, RemoteDMATransfer
+from concourse.mybir import AluOpType, AxisListType, ActivationFunctionType
+
+N, TC, CAP = 8, 1024, 256
+W = CAP + 8
+LW = N * W + 8
+BIG = 1024.0
+NS = 90
+
+SCRATCH = {
+    "X": ("sbuf", [128, TC], "bfloat16"),
+    "land": ("sbuf", [128, LW], "bfloat16"),
+    "Yb": ("sbuf", [128, N * CAP], "bfloat16"),
+    "K16": ("sbuf", [128, 64], "int32"),
+    "Kf": ("sbuf", [128, 66], "float16"),
+    "Z": ("sbuf", [128, 66], "float32"),
+    "PI": ("sbuf", [128, 4], "int32"),
+    "PF": ("sbuf", [128, 12], "float32"),
+    "iI": ("sbuf", [128, 128], "float32"),
+    "iT": ("sbuf", [128, 128], "float32"),
+    "iC": ("sbuf", [128, 64], "float32"),
+    "iG": ("sbuf", [128, 16], "float32"),
+    "G16": ("sbuf", [128, 128], "float32"),
+    "E16": ("sbuf", [128, 128], "float32"),
+    "LA": ("sbuf", [128, 128], "float16"),
+    "LB": ("sbuf", [128, 128], "float16"),
+    "TR": ("sbuf", [128, 64], "float32"),
+    "selU": ("sbuf", [128, 1], "uint16"),
+    "val": ("sbuf", [128, 128], "bfloat16"),
+    "R1": ("sbuf", [128, 8], "bfloat16"),
+    "M1": ("sbuf", [128, 16], "float32"),
+    "Am": ("sbuf", [128, 128], "float16"),
+    "Vv": ("sbuf", [128, 65], "float32"),
+    "Vm": ("sbuf", [128, 72], "float32"),
+    "dst16": ("sbuf", [128, 16], "uint16"),
+    "Wn": ("sbuf", [128, 384], "bfloat16"),
+    "Bm": ("sbuf", [128, 16], "float16"),
+    "idxU": ("sbuf", [128, 16], "uint16"),
+    "cidx": ("sbuf", [128, 128], "float16"),
+    "C0": ("sbuf", [128, 128], "float16"),
+    "Tt": ("sbuf", [128, 128], "float16"),
+    "offs": ("sbuf", [128, 128], "uint16"),
+    "junk": ("sbuf", [128, 8], "float32"),
+    "pD": ("psum", [128, 512], "float32"),
+    "p1": ("psum", [128, 512], "float32"),
+    "p2": ("psum", [128, 512], "float32"),
+    "pL": ("psum", [128, 512], "float32"),
+}
+SEMAPHORES = ["s%d" % i for i in range(NS)] + ["arr%d" % b for b in range(N)] + ["sent"]
+
+
+def rank_program(g, core, T, topo):
+    rank = T.rank_of(core)
+    if rank is None:
+        return
+    V, S, P, Y = g.vector, g.scalar, g.tensor, g.sync
+    OP, FN = AluOpType, ActivationFunctionType
+    nsem, seen, open_h = [0], {}, {}
+
+    def done(ins, n=1):
+        h = ("s%d" % nsem[0], n)
+        nsem[0] += 1
+        ins.then_inc(T.sem[h[0]], n)
+        open_h[h] = 1
+        return h
+
+    def need(q, *hs):
+        for h in hs:
+            if (q[0], h) not in seen:
+                seen[(q[0], h)] = 1
+                q[1].wait_ge(T.sem[h[0]], h[1])
+                open_h.pop(h, None)
+
+    qG, qV, qS, qP, qY = ("g", g), ("v", V), ("s", S), ("p", P), ("y", Y)
+
+    def col(j):
+        return T.PF[:, j:j + 1]
+    pf, pdiv, pmod, ca, cb, ctmp, crr, cge, ceq, ca0, cSp, cgp = [col(j) for j in range(12)]
+
+    def ts(deps, out, in0, s1, s2, op0, op1=None):
+        need(qV, *deps)
+        if op1 is None:
+            return done(V.tensor_scalar(out, in0, s1, None, op0))
+        return done(V.tensor_scalar(out, in0, s1, s2, op0, op1))
+
+    def tt(deps, out, in0, in1, op):
+        need(qV, *deps)
+        return done(V.tensor_tensor(out, in0, in1, op))
+
+    def cp(deps, out, in_):
+        need(qV, *deps)
+        return done(V.tensor_copy(out, in_))
+
+    def act(deps, out, in_, func, **kw):
+        need(qS, *deps)
+        return done(S.activation(out, in_, func, **kw))
+
+    def mm(deps, out, lhsT, rhs, start, stop):
+        need(qP, *deps)
+        return done(P.matmul(out, lhsT, rhs, start, stop))
+
+    def blk(b):
+        return T.land[:, b * W:(b + 1) * W]
+    own = rank * W
+
+    others = [c for c in T.cores if c != core]
+    peers = [c for c in others if topo.same_plane(core, c)]
+    partner = [c for c in others if topo.rack(topo.host(c)) != topo.rack(topo.host(core))
+               and topo.may_write(core, c) and topo.chip(c) == topo.chip(core)][0]
+    prank = T.rank_of(partner)
+
+    dK = done(Y.dma_start(T.K16[0:16, :], T.keep[:, :]), 16)
+    dX = done(S.dma_start(T.X[:, :], T.x[:, :]), 16)
+
+    hP = done(g.iota(T.PI[:, 0:1], [[0, 1]], 0, 1))
+    hI = done(g.iota(T.iI[:, :], [[0, 8], [1, 16]], 0, 0, allow_small_or_imprecise_dtypes=True))
+    hC = done(g.iota(T.iC[:, :], [[0, 8], [16, 8]], CAP, 0, allow_small_or_imprecise_dtypes=True))
+    hT = done(g.iota(T.iT[:, :], [[1, 128]], 0, 0, allow_small_or_imprecise_dtypes=True))
+    hG = done(g.iota(T.iG[:, :], [[0, 2], [1, 8]], 0, 0, allow_small_or_imprecise_dtypes=True))
+
+    mZ = done(V.memset(T.Z[:, :], 0.0))
+    mW = done(V.memset(T.Wn[:, :], 0.0))
+    mV = done(V.memset(T.Vm[:, 64:72], 0.0))
+    mP = done(V.memset(T.land[:, own + CAP + 2:own + W], 0.0))
+    m0 = done(V.memset(T.land[:, N * W:LW], 0.0))
+    kz = cp([mZ], T.Kf[0:16, :], T.Z[0:16, :])
+
+    h = ts([hP], T.PI[:, 2:3], T.PI[:, 0:1], 15, None, OP.bitwise_and)
+    hmod = cp([h], pmod, T.PI[:, 2:3])
+    hg16 = ts([hI, hmod], T.G16[0:16, :], T.iI[0:16, :], T.PF[0:16, 2:3], None, OP.is_gt)
+    he16 = ts([], T.E16[0:16, :], T.iI[0:16, :], T.PF[0:16, 2:3], -BIG, OP.is_equal, OP.mult)
+    hLA = tt([hg16, he16], T.LA[0:16, :], T.G16[0:16, :], T.E16[0:16, :], OP.add)
+    hLB = ts([hLA], T.LB[0:16, :], T.LA[0:16, :], -1.0, 1.0, OP.mult, OP.add)
+    hTR = act([hC, hmod], T.TR[:, :], T.iC[:, :], FN.Identity, bias=pmod, scale=1.0)
+    h = ts([], T.PI[:, 1:2], T.PI[:, 0:1], 4, None, OP.arith_shift_right)
+    hdiv = cp([h], pdiv, T.PI[:, 1:2])
+    hpf = cp([], pf, T.PI[:, 0:1])
+    hsel = ts([hdiv, hpf], T.selU[:, :], pdiv, -8.0, pf, OP.mult, OP.add)
+    ha = ts([], ca, pmod, 0.0, None, OP.is_equal)
+    hb = ts([], cb, pmod, 1.0, None, OP.is_equal)
+    hval = act([hT, ha, hb], T.val[:, :], T.iT[:, :], FN.Identity, bias=cb, scale=ca)
+    h = ts([], ctmp, pf, -1.0, 8.0, OP.add, OP.mult)
+    hrr = ts([h, ha, hb], crr, ctmp, cb, ca, OP.mult, OP.add)
+    hR1 = act([hG, hrr], T.R1[:, :], T.iG[:, 0:8], FN.Identity, bias=crr, scale=0.0)
+    hM1 = ts([hG], T.M1[:, :], T.iG[:, :], pdiv, None, OP.is_equal)
+    hAm = ts([], T.Am[:, :], T.iI[:, :], pmod, None, OP.is_equal)
+    hge = ts([], cge, pdiv, float(rank), None, OP.is_ge)
+    heq = ts([], ceq, pdiv, float(rank), None, OP.is_equal)
+
+    hk = cp([dK, kz], T.Kf[0:16, 1:65], T.K16[0:16, :])
+    mm([hk, hLA], T.pD[:, 0:65], T.LA[0:16, :], T.Kf[0:16, 1:66], True, False)
+    hD = mm([hLB], T.pD[:, 0:65], T.LB[0:16, :], T.Kf[0:16, 0:65], False, True)
+    need(qV, hD)
+    hV = done(V.tensor_tensor_scan(T.Vv[:, :], T.pD[:, 0:65], T.Z[:, 0:65], BIG, OP.add, OP.add))
+    hVm = tt([hV, hTR], T.Vm[:, 0:64], T.Vv[:, 0:64], T.TR[:, :], OP.min)
+    hds = cp([hVm, mV, hsel], T.dst16[:, :], T.Vm[:, 0:72].indirect(T.selU[:, 0:1]))
+    hsc = cp([hds, mW, hval], T.Wn[:, 0:384].indirect(T.dst16[:, 0:8]), T.val[:, :])
+    hc0 = ts([hge], T.land[:, own + CAP:own + CAP + 1], T.Vv[:, 64:65], -BIG, cge, OP.add, OP.mult)
+    hc1 = ts([heq], T.land[:, own + CAP + 1:own + CAP + 2], T.Vv[:, 64:65], -BIG, ceq, OP.add, OP.mult)
+    mm([hsc, hR1], T.p1[:, 0:8], T.Wn[:, 0:128], T.R1[:, :], True, True)
+    h1 = mm([], T.p1[:, 8:16], T.Wn[:, 128:256], T.R1[:, :], True, True)
+    hB = tt([h1, hM1], T.Bm[:, :], T.p1[:, 0:16], T.M1[:, :], OP.mult)
+    h2 = mm([hB, hAm], T.p2[:, 0:16], T.Am[:, :], T.Bm[:, :], True, True)
+    hix = cp([h2], T.idxU[:, :], T.p2[:, 0:16])
+
+    hgS = act([hix, dX], T.land[:, own + 128:own + 256], T.X[:, :].indirect(T.idxU[:, 8:16]), FN.Copy)
+    hgV = cp([hix, dX], T.land[:, own:own + 128], T.X[:, :].indirect(T.idxU[:, 0:8]))
+
+    def eng(m):
+        return bin(m).count("1")
+
+    def fan(b, dests):
+        m = topo.mask(core, dests[0])
+        ids = []
+        for d in dests:
+            m &= topo.mask(core, d)
+            rid, pid = topo.addr(d, core)
+            ids.append(DstId(rid=rid, pnc=pid))
+        g.remote_dma_fused([RemoteDMATransfer(dst_ids=ids, dma_engine_mask=m, remote_sem=T.sem["arr%d" % b],
+                                              srcs=[blk(b)], dsts=[blk(b) for d in dests])], local_sem=T.sem.sent)
+        return eng(m)
+
+    need(qG, hgV, hgS, hc0, hc1, mP)
+    sent = fan(rank, [partner])
+    sent += fan(rank, peers)
+    ne = eng(topo.mask(partner, core))
+    g.wait_ge(T.sem["arr%d" % prank], ne)
+    sent += fan(prank, peers)
+
+    hci = ts([hT], T.cidx[:, :], T.iT[:, :], 16.0, pmod, OP.mult, OP.add)
+    h = ts([], ca0, pdiv, 0.0, None, OP.is_equal)
+    hC0 = ts([hci, h], T.C0[:, :], T.cidx[:, :], ca0, None, OP.mult)
+    mm([hC0], T.pL[:, 0:128], T.Am[:, :], T.C0[:, :], True, False)
+
+    for b in range(N):
+        if b != rank:
+            V.wait_ge(T.sem["arr%d" % b], ne)
+            S.wait_ge(T.sem["arr%d" % b], ne)
+    mine = [m0, mP, hgV, hgS, hc0, hc1]
+    need(qV, *mine)
+    hSp = done(V.tensor_reduce(cSp, T.land[:, CAP:CAP + (N - 1) * W + 1:W], AxisListType.X, OP.add))
+    hgp = act(mine, T.junk[:, :], T.land[:, CAP + 1:CAP + 1 + (N - 1) * W + 1:W], FN.Identity,
+              bias=float(W // N), scale=-1.0, accum_out=cgp)
+    hTt = ts([hSp, hgp], T.Tt[:, :], T.cidx[:, :], cSp, cgp, OP.is_ge, OP.mult)
+    hL = mm([hTt], T.pL[:, 0:128], T.Am[:, :], T.Tt[:, :], False, True)
+    hoA = ts([hL], T.offs[:, 0:64], T.pL[:, 0:64], float(N * W), None, OP.min)
+    hoB = ts([], T.offs[:, 64:128], T.pL[:, 64:128], float(N * W), None, OP.min)
+    win = T.land[:, 0:LW]
+    s0 = act([hoA], T.Yb[:, 0:512], win.indirect(T.offs[:, 0:32]), FN.Copy)
+    v0 = cp([hoA], T.Yb[:, 512:1024], win.indirect(T.offs[:, 32:64]))
+    s1 = act([hoB], T.Yb[:, 1024:1536], win.indirect(T.offs[:, 64:96]), FN.Copy)
+    v1 = cp([hoB], T.Yb[:, 1536:2048], win.indirect(T.offs[:, 96:128]))
+    need(qY, s0, v0)
+    st0 = done(Y.dma_start(T.y[:, 0:1024], T.Yb[:, 0:1024]), 16)
+    need(qY, s1, v1)
+    st1 = done(Y.dma_start(T.y[:, 1024:2048], T.Yb[:, 1024:2048]), 16)
+    need(qY, st0, st1)
+    g.wait_ge(T.sem.sent, sent)
+    need(qG, *list(open_h))

@@ -5,25 +5,31 @@ N, TC, CAP = 8, 1024, 256
 W = CAP + 8
 LW = N * W + 8
 BIG = 1024.0
-NS = 90
+NS = 100
 
 SCRATCH = {
     "X": ("sbuf", [128, TC], "bfloat16"),
     "land": ("sbuf", [128, LW], "bfloat16"),
     "Yb": ("sbuf", [128, N * CAP], "bfloat16"),
+    "kall": ("dram", [N * 128, 8], "int32"),
+    "KA": ("sbuf", [128, 64], "int32"),
+    "KAf": ("sbuf", [128, 64], "float32"),
     "K16": ("sbuf", [128, 64], "int32"),
     "Kf": ("sbuf", [128, 66], "float16"),
     "Z": ("sbuf", [128, 66], "float32"),
     "PI": ("sbuf", [128, 4], "int32"),
-    "PF": ("sbuf", [128, 12], "float32"),
+    "PF": ("sbuf", [128, 16], "float32"),
     "iI": ("sbuf", [128, 128], "float32"),
     "iT": ("sbuf", [128, 128], "float32"),
+    "iD": ("sbuf", [128, 128], "float32"),
     "iC": ("sbuf", [128, 64], "float32"),
     "iG": ("sbuf", [128, 16], "float32"),
     "G16": ("sbuf", [128, 128], "float32"),
     "E16": ("sbuf", [128, 128], "float32"),
     "LA": ("sbuf", [128, 128], "float16"),
     "LB": ("sbuf", [128, 128], "float16"),
+    "MLE": ("sbuf", [128, 128], "float32"),
+    "MEQ": ("sbuf", [128, 128], "float32"),
     "TR": ("sbuf", [128, 64], "float32"),
     "selU": ("sbuf", [128, 1], "uint16"),
     "val": ("sbuf", [128, 128], "bfloat16"),
@@ -37,6 +43,7 @@ SCRATCH = {
     "Bm": ("sbuf", [128, 16], "float16"),
     "idxU": ("sbuf", [128, 16], "uint16"),
     "cidx": ("sbuf", [128, 128], "float16"),
+    "cid2": ("sbuf", [128, 128], "float16"),
     "C0": ("sbuf", [128, 128], "float16"),
     "Tt": ("sbuf", [128, 128], "float16"),
     "offs": ("sbuf", [128, 128], "uint16"),
@@ -45,8 +52,9 @@ SCRATCH = {
     "p1": ("psum", [128, 512], "float32"),
     "p2": ("psum", [128, 512], "float32"),
     "pL": ("psum", [128, 512], "float32"),
+    "pS": ("psum", [128, 512], "float32"),
 }
-SEMAPHORES = ["s%d" % i for i in range(NS)] + ["arr%d" % b for b in range(N)] + ["sent"]
+SEMAPHORES = ["s%d" % i for i in range(NS)] + ["arr%d" % b for b in range(N)] + ["sent", "kin"]
 
 
 def rank_program(g, core, T, topo):
@@ -75,7 +83,7 @@ def rank_program(g, core, T, topo):
 
     def col(j):
         return T.PF[:, j:j + 1]
-    pf, pdiv, pmod, ca, cb, ctmp, crr, cge, ceq, ca0, cSp, cgp = [col(j) for j in range(12)]
+    pf, pdiv, pmod, ca, cb, ctmp, crr, crs, cge, ceq, ca0, cgp, cSp, cbi = [col(j) for j in range(14)]
 
     def ts(deps, out, in0, s1, s2, op0, op1=None):
         need(qV, *deps)
@@ -101,6 +109,9 @@ def rank_program(g, core, T, topo):
 
     def blk(b):
         return T.land[:, b * W:(b + 1) * W]
+
+    def ktab(b):
+        return T.kall[b * 128:(b + 1) * 128, :]
     own = rank * W
 
     others = [c for c in T.cores if c != core]
@@ -109,7 +120,24 @@ def rank_program(g, core, T, topo):
                and topo.may_write(core, c) and topo.chip(c) == topo.chip(core)][0]
     prank = T.rank_of(partner)
 
+    def eng(m):
+        return bin(m).count("1")
+    ne = eng(topo.mask(partner, core))
+    sent = [0]
+
+    def fan(piece, dests, sem):
+        m = topo.mask(core, dests[0])
+        ids = []
+        for d in dests:
+            m &= topo.mask(core, d)
+            rid, pid = topo.addr(d, core)
+            ids.append(DstId(rid=rid, pnc=pid))
+        g.remote_dma_fused([RemoteDMATransfer(dst_ids=ids, dma_engine_mask=m, remote_sem=sem,
+                                              srcs=[piece], dsts=[piece for d in dests])], local_sem=T.sem.sent)
+        sent[0] += eng(m)
+
     dK = done(Y.dma_start(T.K16[0:16, :], T.keep[:, :]), 16)
+    dKD = done(Y.dma_start(ktab(rank), T.keep[:, :]), 16)
     dX = done(S.dma_start(T.X[:, :], T.x[:, :]), 16)
 
     hP = done(g.iota(T.PI[:, 0:1], [[0, 1]], 0, 1))
@@ -117,6 +145,10 @@ def rank_program(g, core, T, topo):
     hC = done(g.iota(T.iC[:, :], [[0, 8], [16, 8]], CAP, 0, allow_small_or_imprecise_dtypes=True))
     hT = done(g.iota(T.iT[:, :], [[1, 128]], 0, 0, allow_small_or_imprecise_dtypes=True))
     hG = done(g.iota(T.iG[:, :], [[0, 2], [1, 8]], 0, 0, allow_small_or_imprecise_dtypes=True))
+    hDv = done(g.iota(T.iD[:, :], [[1, 8], [0, 16]], 0, 0, allow_small_or_imprecise_dtypes=True))
+
+    need(qG, dKD)
+    fan(ktab(rank), peers, T.sem.kin)
 
     mZ = done(V.memset(T.Z[:, :], 0.0))
     mW = done(V.memset(T.Wn[:, :], 0.0))
@@ -166,42 +198,47 @@ def rank_program(g, core, T, topo):
     hgS = act([hix, dX], T.land[:, own + 128:own + 256], T.X[:, :].indirect(T.idxU[:, 8:16]), FN.Copy)
     hgV = cp([hix, dX], T.land[:, own:own + 128], T.X[:, :].indirect(T.idxU[:, 0:8]))
 
-    def eng(m):
-        return bin(m).count("1")
-
-    def fan(b, dests):
-        m = topo.mask(core, dests[0])
-        ids = []
-        for d in dests:
-            m &= topo.mask(core, d)
-            rid, pid = topo.addr(d, core)
-            ids.append(DstId(rid=rid, pnc=pid))
-        g.remote_dma_fused([RemoteDMATransfer(dst_ids=ids, dma_engine_mask=m, remote_sem=T.sem["arr%d" % b],
-                                              srcs=[blk(b)], dsts=[blk(b) for d in dests])], local_sem=T.sem.sent)
-        return eng(m)
-
     need(qG, hgV, hgS, hc0, hc1, mP)
-    sent = fan(rank, [partner])
-    sent += fan(rank, peers)
-    ne = eng(topo.mask(partner, core))
+    fan(blk(rank), [partner], T.sem["arr%d" % rank])
+    fan(T.land[:, own:own + CAP], peers, T.sem["arr%d" % rank])
     g.wait_ge(T.sem["arr%d" % prank], ne)
-    sent += fan(prank, peers)
+    fan(blk(prank), peers, T.sem["arr%d" % prank])
 
+    mKA = done(V.memset(T.KA[:, :], 0))
+    mine = [m0, mP, hgV, hgS, hc0, hc1]
+    for d in peers:
+        b = T.rank_of(d)
+        mine.append(done(V.memset(T.land[:, b * W + CAP:(b + 1) * W], 0.0)))
     hci = ts([hT], T.cidx[:, :], T.iT[:, :], 16.0, pmod, OP.mult, OP.add)
     h = ts([], ca0, pdiv, 0.0, None, OP.is_equal)
     hC0 = ts([hci, h], T.C0[:, :], T.cidx[:, :], ca0, None, OP.mult)
+    hLE = ts([hDv], T.MLE[:, :], T.iD[:, :], pdiv, None, OP.is_ge)
+    hEQ = ts([], T.MEQ[:, :], T.iD[:, :], pdiv, None, OP.is_equal)
     mm([hC0], T.pL[:, 0:128], T.Am[:, :], T.C0[:, :], True, False)
+
+    Y.wait_ge(T.sem.kin, len(peers) * ne)
+    need(qY, mKA)
+    dKA = []
+    for d in peers:
+        b = T.rank_of(d)
+        dKA.append(done(Y.dma_start(T.KA[16 * b:16 * b + 16, :], ktab(b)), 16))
+    hkf = cp(dKA + [mKA], T.KAf[:, :], T.KA[:, :])
+    need(qV, hkf)
+    hrs = done(V.tensor_reduce(crs, T.KAf[:, :], AxisListType.X, OP.add))
+    hS0 = mm([hrs, hLE], T.pS[:, 0:1], T.MLE[:, :], crs, True, True)
+    hS1 = mm([hEQ], T.pS[:, 1:2], T.MEQ[:, :], crs, True, True)
+    hc2 = ts([hS0, hS1], T.cid2[:, :], T.cidx[:, :], T.pS[:, 0:1], None, OP.subtract)
+    hbi = ts([], cbi, T.pS[:, 1:2], -1.0 / N, float(W // N), OP.mult, OP.add)
 
     for b in range(N):
         if b != rank:
             V.wait_ge(T.sem["arr%d" % b], ne)
             S.wait_ge(T.sem["arr%d" % b], ne)
-    mine = [m0, mP, hgV, hgS, hc0, hc1]
     need(qV, *mine)
     hSp = done(V.tensor_reduce(cSp, T.land[:, CAP:CAP + (N - 1) * W + 1:W], AxisListType.X, OP.add))
-    hgp = act(mine, T.junk[:, :], T.land[:, CAP + 1:CAP + 1 + (N - 1) * W + 1:W], FN.Identity,
-              bias=float(W // N), scale=-1.0, accum_out=cgp)
-    hTt = ts([hSp, hgp], T.Tt[:, :], T.cidx[:, :], cSp, cgp, OP.is_ge, OP.mult)
+    hgp = act(mine + [hbi], T.junk[:, :], T.land[:, CAP + 1:CAP + 1 + (N - 1) * W + 1:W], FN.Identity,
+              bias=cbi, scale=-1.0, accum_out=cgp)
+    hTt = ts([hSp, hgp, hc2], T.Tt[:, :], T.cid2[:, :], cSp, cgp, OP.is_ge, OP.mult)
     hL = mm([hTt], T.pL[:, 0:128], T.Am[:, :], T.Tt[:, :], False, True)
     hoA = ts([hL], T.offs[:, 0:64], T.pL[:, 0:64], float(N * W), None, OP.min)
     hoB = ts([], T.offs[:, 64:128], T.pL[:, 64:128], float(N * W), None, OP.min)
@@ -215,5 +252,5 @@ def rank_program(g, core, T, topo):
     need(qY, s1, v1)
     st1 = done(Y.dma_start(T.y[:, 1024:2048], T.Yb[:, 1024:2048]), 16)
     need(qY, st0, st1)
-    g.wait_ge(T.sem.sent, sent)
+    g.wait_ge(T.sem.sent, sent[0])
     need(qG, *list(open_h))

from concourse.bass import DstId, RemoteDMATransfer
from concourse.mybir import AluOpType, AxisListType, ActivationFunctionType

N, TC, CAP = 8, 1024, 256
W = CAP + 8
LW = N * W + 8
BIG = 1024.0
NS = 100

SCRATCH = {
    "X": ("sbuf", [128, TC], "bfloat16"),
    "land": ("sbuf", [128, LW], "bfloat16"),
    "Yb": ("sbuf", [128, N * CAP], "bfloat16"),
    "kall": ("dram", [N * 128, 8], "int32"),
    "KA": ("sbuf", [128, 64], "int32"),
    "KAf": ("sbuf", [128, 64], "float32"),
    "K16": ("sbuf", [128, 64], "int32"),
    "Kf": ("sbuf", [128, 66], "float16"),
    "Z": ("sbuf", [128, 66], "float32"),
    "PI": ("sbuf", [128, 4], "int32"),
    "PF": ("sbuf", [128, 16], "float32"),
    "iI": ("sbuf", [128, 128], "float32"),
    "iT": ("sbuf", [128, 128], "float32"),
    "iD": ("sbuf", [128, 128], "float32"),
    "iC": ("sbuf", [128, 64], "float32"),
    "iG": ("sbuf", [128, 16], "float32"),
    "G16": ("sbuf", [128, 128], "float32"),
    "E16": ("sbuf", [128, 128], "float32"),
    "LA": ("sbuf", [128, 128], "float16"),
    "LB": ("sbuf", [128, 128], "float16"),
    "MLE": ("sbuf", [128, 128], "float32"),
    "MEQ": ("sbuf", [128, 128], "float32"),
    "TR": ("sbuf", [128, 64], "float32"),
    "selU": ("sbuf", [128, 1], "uint16"),
    "val": ("sbuf", [128, 128], "bfloat16"),
    "R1": ("sbuf", [128, 8], "bfloat16"),
    "M1": ("sbuf", [128, 16], "float32"),
    "Am": ("sbuf", [128, 128], "float16"),
    "Vv": ("sbuf", [128, 65], "float32"),
    "Vm": ("sbuf", [128, 72], "float32"),
    "dst16": ("sbuf", [128, 16], "uint16"),
    "Wn": ("sbuf", [128, 384], "bfloat16"),
    "Bm": ("sbuf", [128, 16], "float16"),
    "idxU": ("sbuf", [128, 16], "uint16"),
    "cidx": ("sbuf", [128, 128], "float16"),
    "cid2": ("sbuf", [128, 128], "float16"),
    "C0": ("sbuf", [128, 128], "float16"),
    "Tt": ("sbuf", [128, 128], "float16"),
    "offs": ("sbuf", [128, 128], "uint16"),
    "junk": ("sbuf", [128, 8], "float32"),
    "pD": ("psum", [128, 512], "float32"),
    "p1": ("psum", [128, 512], "float32"),
    "p2": ("psum", [128, 512], "float32"),
    "pL": ("psum", [128, 512], "float32"),
    "pS": ("psum", [128, 512], "float32"),
}
SEMAPHORES = ["s%d" % i for i in range(NS)] + ["arr%d" % b for b in range(N)] + ["sent", "kin"]


def rank_program(g, core, T, topo):
    rank = T.rank_of(core)
    if rank is None:
        return
    V, S, P, Y = g.vector, g.scalar, g.tensor, g.sync
    OP, FN = AluOpType, ActivationFunctionType
    nsem, seen, open_h = [0], {}, {}

    def done(ins, n=1):
        h = ("s%d" % nsem[0], n)
        nsem[0] += 1
        ins.then_inc(T.sem[h[0]], n)
        open_h[h] = 1
        return h

    def need(q, *hs):
        for h in hs:
            if (q[0], h) not in seen:
                seen[(q[0], h)] = 1
                q[1].wait_ge(T.sem[h[0]], h[1])
                open_h.pop(h, None)

    qG, qV, qS, qP, qY = ("g", g), ("v", V), ("s", S), ("p", P), ("y", Y)

    def col(j):
        return T.PF[:, j:j + 1]
    pf, pdiv, pmod, ca, cb, ctmp, crr, crs, cge, ceq, ca0, cgp, cSp, cbi = [col(j) for j in range(14)]

    def ts(deps, out, in0, s1, s2, op0, op1=None):
        need(qV, *deps)
        if op1 is None:
            return done(V.tensor_scalar(out, in0, s1, None, op0))
        return done(V.tensor_scalar(out, in0, s1, s2, op0, op1))

    def tt(deps, out, in0, in1, op):
        need(qV, *deps)
        return done(V.tensor_tensor(out, in0, in1, op))

    def cp(deps, out, in_):
        need(qV, *deps)
        return done(V.tensor_copy(out, in_))

    def act(deps, out, in_, func, **kw):
        need(qS, *deps)
        return done(S.activation(out, in_, func, **kw))

    def mm(deps, out, lhsT, rhs, start, stop):
        need(qP, *deps)
        return done(P.matmul(out, lhsT, rhs, start, stop))

    def blk(b):
        return T.land[:, b * W:(b + 1) * W]

    def ktab(b):
        return T.kall[b * 128:(b + 1) * 128, :]
    own = rank * W

    others = [c for c in T.cores if c != core]
    peers = [c for c in others if topo.same_plane(core, c)]
    partner = [c for c in others if topo.rack(topo.host(c)) != topo.rack(topo.host(core))
               and topo.may_write(core, c) and topo.chip(c) == topo.chip(core)][0]
    prank = T.rank_of(partner)

    def eng(m):
        return bin(m).count("1")
    ne = eng(topo.mask(partner, core))
    sent = [0]

    def fan(piece, dests, sem):
        m = topo.mask(core, dests[0])
        ids = []
        for d in dests:
            m &= topo.mask(core, d)
            rid, pid = topo.addr(d, core)
            ids.append(DstId(rid=rid, pnc=pid))
        g.remote_dma_fused([RemoteDMATransfer(dst_ids=ids, dma_engine_mask=m, remote_sem=sem,
                                              srcs=[piece], dsts=[piece for d in dests])], local_sem=T.sem.sent)
        sent[0] += eng(m)

    dK = done(Y.dma_start(T.K16[0:16, :], T.keep[:, :]), 16)
    dKD = done(Y.dma_start(ktab(rank), T.keep[:, :]), 16)
    dX = done(S.dma_start(T.X[:, :], T.x[:, :]), 16)

    hP = done(g.iota(T.PI[:, 0:1], [[0, 1]], 0, 1))
    hI = done(g.iota(T.iI[:, :], [[0, 8], [1, 16]], 0, 0, allow_small_or_imprecise_dtypes=True))
    hC = done(g.iota(T.iC[:, :], [[0, 8], [16, 8]], CAP, 0, allow_small_or_imprecise_dtypes=True))
    hT = done(g.iota(T.iT[:, :], [[1, 128]], 0, 0, allow_small_or_imprecise_dtypes=True))
    hG = done(g.iota(T.iG[:, :], [[0, 2], [1, 8]], 0, 0, allow_small_or_imprecise_dtypes=True))
    hDv = done(g.iota(T.iD[:, :], [[1, 8], [0, 16]], 0, 0, allow_small_or_imprecise_dtypes=True))

    need(qG, dKD)
    fan(ktab(rank), peers, T.sem.kin)

    mZ = done(V.memset(T.Z[:, :], 0.0))
    mW = done(V.memset(T.Wn[:, :], 0.0))
    mV = done(V.memset(T.Vm[:, 64:72], 0.0))
    mP = done(V.memset(T.land[:, own + CAP + 2:own + W], 0.0))
    m0 = done(V.memset(T.land[:, N * W:LW], 0.0))
    kz = cp([mZ], T.Kf[0:16, :], T.Z[0:16, :])

    h = ts([hP], T.PI[:, 2:3], T.PI[:, 0:1], 15, None, OP.bitwise_and)
    hmod = cp([h], pmod, T.PI[:, 2:3])
    hg16 = ts([hI, hmod], T.G16[0:16, :], T.iI[0:16, :], T.PF[0:16, 2:3], None, OP.is_gt)
    he16 = ts([], T.E16[0:16, :], T.iI[0:16, :], T.PF[0:16, 2:3], -BIG, OP.is_equal, OP.mult)
    hLA = tt([hg16, he16], T.LA[0:16, :], T.G16[0:16, :], T.E16[0:16, :], OP.add)
    hLB = ts([hLA], T.LB[0:16, :], T.LA[0:16, :], -1.0, 1.0, OP.mult, OP.add)
    hTR = act([hC, hmod], T.TR[:, :], T.iC[:, :], FN.Identity, bias=pmod, scale=1.0)
    h = ts([], T.PI[:, 1:2], T.PI[:, 0:1], 4, None, OP.arith_shift_right)
    hdiv = cp([h], pdiv, T.PI[:, 1:2])
    hpf = cp([], pf, T.PI[:, 0:1])
    hsel = ts([hdiv, hpf], T.selU[:, :], pdiv, -8.0, pf, OP.mult, OP.add)
    ha = ts([], ca, pmod, 0.0, None, OP.is_equal)
    hb = ts([], cb, pmod, 1.0, None, OP.is_equal)
    hval = act([hT, ha, hb], T.val[:, :], T.iT[:, :], FN.Identity, bias=cb, scale=ca)
    h = ts([], ctmp, pf, -1.0, 8.0, OP.add, OP.mult)
    hrr = ts([h, ha, hb], crr, ctmp, cb, ca, OP.mult, OP.add)
    hR1 = act([hG, hrr], T.R1[:, :], T.iG[:, 0:8], FN.Identity, bias=crr, scale=0.0)
    hM1 = ts([hG], T.M1[:, :], T.iG[:, :], pdiv, None, OP.is_equal)
    hAm = ts([], T.Am[:, :], T.iI[:, :], pmod, None, OP.is_equal)
    hge = ts([], cge, pdiv, float(rank), None, OP.is_ge)
    heq = ts([], ceq, pdiv, float(rank), None, OP.is_equal)

    hk = cp([dK, kz], T.Kf[0:16, 1:65], T.K16[0:16, :])
    mm([hk, hLA], T.pD[:, 0:65], T.LA[0:16, :], T.Kf[0:16, 1:66], True, False)
    hD = mm([hLB], T.pD[:, 0:65], T.LB[0:16, :], T.Kf[0:16, 0:65], False, True)
    need(qV, hD)
    hV = done(V.tensor_tensor_scan(T.Vv[:, :], T.pD[:, 0:65], T.Z[:, 0:65], BIG, OP.add, OP.add))
    hVm = tt([hV, hTR], T.Vm[:, 0:64], T.Vv[:, 0:64], T.TR[:, :], OP.min)
    hds = cp([hVm, mV, hsel], T.dst16[:, :], T.Vm[:, 0:72].indirect(T.selU[:, 0:1]))
    hsc = cp([hds, mW, hval], T.Wn[:, 0:384].indirect(T.dst16[:, 0:8]), T.val[:, :])
    hc0 = ts([hge], T.land[:, own + CAP:own + CAP + 1], T.Vv[:, 64:65], -BIG, cge, OP.add, OP.mult)
    hc1 = ts([heq], T.land[:, own + CAP + 1:own + CAP + 2], T.Vv[:, 64:65], -BIG, ceq, OP.add, OP.mult)
    mm([hsc, hR1], T.p1[:, 0:8], T.Wn[:, 0:128], T.R1[:, :], True, True)
    h1 = mm([], T.p1[:, 8:16], T.Wn[:, 128:256], T.R1[:, :], True, True)
    hB = tt([h1, hM1], T.Bm[:, :], T.p1[:, 0:16], T.M1[:, :], OP.mult)
    h2 = mm([hB, hAm], T.p2[:, 0:16], T.Am[:, :], T.Bm[:, :], True, True)
    hix = cp([h2], T.idxU[:, :], T.p2[:, 0:16])

    hgS = act([hix, dX], T.land[:, own + 128:own + 256], T.X[:, :].indirect(T.idxU[:, 8:16]), FN.Copy)
    hgV = cp([hix, dX], T.land[:, own:own + 128], T.X[:, :].indirect(T.idxU[:, 0:8]))

    need(qG, hgV, hgS, hc0, hc1, mP)
    fan(blk(rank), [partner], T.sem["arr%d" % rank])
    fan(T.land[:, own:own + CAP], peers, T.sem["arr%d" % rank])
    g.wait_ge(T.sem["arr%d" % prank], ne)
    fan(blk(prank), peers, T.sem["arr%d" % prank])

    mKA = done(V.memset(T.KA[:, :], 0))
    mine = [m0, mP, hgV, hgS, hc0, hc1]
    for d in peers:
        b = T.rank_of(d)
        mine.append(done(V.memset(T.land[:, b * W + CAP:(b + 1) * W], 0.0)))
    hci = ts([hT], T.cidx[:, :], T.iT[:, :], 16.0, pmod, OP.mult, OP.add)
    h = ts([], ca0, pdiv, 0.0, None, OP.is_equal)
    hC0 = ts([hci, h], T.C0[:, :], T.cidx[:, :], ca0, None, OP.mult)
    hLE = ts([hDv], T.MLE[:, :], T.iD[:, :], pdiv, None, OP.is_ge)
    hEQ = ts([], T.MEQ[:, :], T.iD[:, :], pdiv, None, OP.is_equal)
    mm([hC0], T.pL[:, 0:128], T.Am[:, :], T.C0[:, :], True, False)

    Y.wait_ge(T.sem.kin, len(peers) * ne)
    need(qY, mKA)
    dKA = []
    for d in peers:
        b = T.rank_of(d)
        dKA.append(done(Y.dma_start(T.KA[16 * b:16 * b + 16, :], ktab(b)), 16))
    hkf = cp(dKA + [mKA], T.KAf[:, :], T.KA[:, :])
    need(qV, hkf)
    hrs = done(V.tensor_reduce(crs, T.KAf[:, :], AxisListType.X, OP.add))
    hS0 = mm([hrs, hLE], T.pS[:, 0:1], T.MLE[:, :], crs, True, True)
    hS1 = mm([hEQ], T.pS[:, 1:2], T.MEQ[:, :], crs, True, True)
    hc2 = ts([hS0, hS1], T.cid2[:, :], T.cidx[:, :], T.pS[:, 0:1], None, OP.subtract)
    hbi = ts([], cbi, T.pS[:, 1:2], -1.0 / N, float(W // N), OP.mult, OP.add)

    for b in range(N):
        if b != rank:
            V.wait_ge(T.sem["arr%d" % b], ne)
            S.wait_ge(T.sem["arr%d" % b], ne)
    need(qV, *mine)
    hSp = done(V.tensor_reduce(cSp, T.land[:, CAP:CAP + (N - 1) * W + 1:W], AxisListType.X, OP.add))
    hgp = act(mine + [hbi], T.junk[:, :], T.land[:, CAP + 1:CAP + 1 + (N - 1) * W + 1:W], FN.Identity,
              bias=cbi, scale=-1.0, accum_out=cgp)
    hTt = ts([hSp, hgp, hc2], T.Tt[:, :], T.cid2[:, :], cSp, cgp, OP.is_ge, OP.mult)
    hL = mm([hTt], T.pL[:, 0:128], T.Am[:, :], T.Tt[:, :], False, True)
    hoA = ts([hL], T.offs[:, 0:64], T.pL[:, 0:64], float(N * W), None, OP.min)
    hoB = ts([], T.offs[:, 64:128], T.pL[:, 64:128], float(N * W), None, OP.min)
    win = T.land[:, 0:LW]
    s0 = act([hoA], T.Yb[:, 0:512], win.indirect(T.offs[:, 0:32]), FN.Copy)
    v0 = cp([hoA], T.Yb[:, 512:1024], win.indirect(T.offs[:, 32:64]))
    s1 = act([hoB], T.Yb[:, 1024:1536], win.indirect(T.offs[:, 64:96]), FN.Copy)
    v1 = cp([hoB], T.Yb[:, 1536:2048], win.indirect(T.offs[:, 96:128]))
    need(qY, s0, v0)
    st0 = done(Y.dma_start(T.y[:, 0:1024], T.Yb[:, 0:1024]), 16)
    need(qY, s1, v1)
    st1 = done(Y.dma_start(T.y[:, 1024:2048], T.Yb[:, 1024:2048]), 16)
    need(qY, st0, st1)
    g.wait_ge(T.sem.sent, sent[0])
    need(qG, *list(open_h))
